import numpy as np
import ml_dtypes


def mxq(x, axis, fmt="e4m3"):
    dtype, down = {"e4m3": (ml_dtypes.float8_e4m3fn, 7), "e5m2": (ml_dtypes.float8_e5m2, 14)}[fmt]
    v = np.moveaxis(np.asarray(x, np.float32).astype(ml_dtypes.bfloat16).astype(np.float64), axis, -1)
    blocks = v.reshape(v.shape[:-1] + (-1, 32))
    amax = np.abs(blocks).max(-1, keepdims=True)
    byte = np.maximum(np.where(amax > 0, np.frexp(amax)[1] - 1 + 127, 0) - down, 1)
    scale = np.exp2(byte - 127.0)
    codes = (blocks / scale).astype(np.float32).astype(dtype).astype(np.float64)
    return np.moveaxis((codes * scale).reshape(v.shape), -1, axis)


WIDE = False


def mx_kscale(k):
    if not WIDE:
        return np.ones(k)
    levels = np.array([10, -10, 5, -5, 0])
    if k % 512:
        return np.exp2(np.random.permutation(np.resize(levels, k // 32))).repeat(32)
    a = np.empty((k // 512, 16))
    for p in range(k // 512):
        a[p, :8] = np.random.permutation(np.resize(levels, 8))
        for g in range(8):
            far = levels[np.abs(levels - a[p, g]) >= 10]
            a[p, g + 8] = far[np.random.randint(len(far))]
    return np.exp2(a.ravel()).repeat(32)


def f64(x):
    return np.asarray(x).astype(np.float64)


def striped(idx):
    return np.tile(idx.reshape(-1, 16).T, (8, 1)).astype(np.uint16)


def unstriped(offs):
    return offs[:16].T.reshape(-1).astype(np.int64)


E2M1 = np.array([0.0, 0.5, 1.0, 1.5, 2.0, 3.0, 4.0, 6.0, -0.0, -0.5, -1.0, -1.5, -2.0, -3.0, -4.0, -6.0])


def pack_weight(w, fmt):
    k, n = w.shape
    w = f64(np.asarray(w, np.float32).astype(ml_dtypes.bfloat16)).reshape(k // 32, 32, n)
    amax = np.abs(w).max(1)
    if fmt == "e4m3":
        byte = np.frexp(amax)[1] - 1 + 127 - 7
    else:
        mant, ex = np.frexp(amax / 6.0)
        byte = np.where(mant > 0.5, ex, ex - 1) + 127
    byte = np.clip(np.where(amax > 0, byte, 1), 1, 254)
    scaled = (w * np.exp2(127.0 - byte)[:, None, :]).reshape(k, n).astype(np.float32)
    by_word = np.ascontiguousarray(scaled.reshape(k // 512, 128, 4, n).transpose(0, 1, 3, 2))
    if fmt == "e4m3":
        words = by_word.astype(ml_dtypes.float8_e4m3fn).view(np.uint8)
    else:
        c = by_word.astype(ml_dtypes.float4_e2m1fn).view(np.uint8) & 0xF
        words = (c[..., 0::2] | (c[..., 1::2] << 4)).reshape(k // 512, 128, 2 * n)
    return np.ascontiguousarray(words), np.ascontiguousarray(byte.astype(np.uint8).reshape(k // 512, 16, n))


def unpack_weight(words, scales, fmt):
    g, _, n = scales.shape
    words = np.ascontiguousarray(words).reshape(g, 128, n, -1)
    if fmt == "e4m3":
        vals = words.view(ml_dtypes.float8_e4m3fn).astype(np.float64)
    else:
        nib = np.empty((g, 128, n, 4), np.uint8)
        nib[..., 0::2] = words & 0xF
        nib[..., 1::2] = words >> 4
        vals = E2M1[nib]
    vals = vals * np.repeat(np.exp2(scales.astype(np.float64) - 127.0), 8, axis=1)[..., None]
    return vals.transpose(0, 1, 3, 2).reshape(g * 512, n)


def gelu(v):
    return 0.5 * v * (1.0 + np.tanh(np.sqrt(2.0 / np.pi) * (v + 0.044715 * v**3)))


def twice(P):
    return np.random.permutation(np.repeat(np.arange(P), 2))


K, H, T, S, P = 1024, 1024, 4096, 1024, 512


def setup_inputs():
    n = np.random.standard_normal
    s = mx_kscale(K)[:, None]
    u = mx_kscale(H)[:, None]
    d = {}
    d["tab_words"], d["tab_scales"] = pack_weight(n((K, T)) * s, "e4m3")
    d["offs"] = striped(np.random.permutation(T)[:S])
    d["pos1"] = striped(np.random.permutation(S)[:P])
    d["pos2"] = striped(np.random.permutation(S)[:P])
    d["pos3"] = striped(twice(P))
    d["wc"] = (0.8 * n((K, H)) / K ** 0.5 / s).astype(np.float32)
    d["ctx"] = (0.8 * n((H, S))).astype(np.float32)
    d["wh_words"], d["wh_scales"] = pack_weight(n((K, H)) / K ** 0.5 / s * u.T, "e2m1")
    d["wy"] = (1.3 * n((H, H)) / H ** 0.5 / u).astype(np.float32)
    d["gain"] = (np.exp(0.3 * n(H)) / u[:, 0]).astype(np.float32)
    return d


def reference(tab_words, tab_scales, offs, pos1, pos2, pos3, wc, ctx, wh_words, wh_scales, wy, gain):
    v = unpack_weight(tab_words, tab_scales, "e4m3")[:, unstriped(offs)]
    wh = unpack_weight(wh_words, wh_scales, "e2m1")
    look = (mxq(f64(wc), 0, "e4m3").T @ v) + f64(ctx)
    h = wh.T @ v
    z = np.maximum(h[:, unstriped(pos1)], h[:, unstriped(pos2)])
    y = mxq(f64(wy), 0, "e4m3").T @ mxq(z, 0, "e4m3")
    hs = h * f64(gain)[:, None]
    return y[:, unstriped(pos3)] * np.tanh(look + hs) + hs

@@ -1,0 +1,286 @@
+from contextlib import ExitStack
+
+import concourse.mybir as mybir
+from concourse.masks import make_identity
+
+K, H, T, S, M = 1024, 1024, 4096, 1024, 512
+FLOPS = 2 * K * H * S * 2 + 2 * H * H * M
+
+F32 = mybir.dt.float32
+BF16 = mybir.dt.bfloat16
+I32 = mybir.dt.int32
+U32 = mybir.dt.uint32
+U16 = mybir.dt.uint16
+U8 = mybir.dt.uint8
+FP8X4 = mybir.dt.float8_e4m3fn_x4
+FP4X4 = mybir.dt.float4_e2m1fn_x4
+ALU = mybir.AluOpType
+ACT = mybir.ActivationFunctionType
+
+P = 128
+PACK = 4
+PASSES = 2
+TILES = 8
+HALF = 512
+Y_PAD = 16
+Y_RING = 4
+ROUTES = "VVMSSSSS"
+
+
+def tile_list_capsule_bleeding_features_kernel(
+    tc, tab_words, tab_scales, offs, pos1, pos2, pos3, wc, ctx, wh_words, wh_scales, wy, gain, out
+):
+    nc = tc.nc
+    with ExitStack() as stack:
+        lists = stack.enter_context(tc.tile_pool(name="lists", bufs=1))
+        sb = stack.enter_context(tc.tile_pool(name="sb", bufs=1))
+        psum = stack.enter_context(tc.psum_pool(name="psum", bufs=1))
+
+        offs_sb = lists.tile([P, S // 16], U16, name="offs_sb")
+        pos1_sb = lists.tile([P, M // 16], U16, name="pos1_sb")
+        pos2_sb = lists.tile([P, M // 16], U16, name="pos2_sb")
+        pos3_sb = lists.tile([P, S // 16], U16, name="pos3_sb")
+
+        tab_planes = sb.tile([P, PASSES * T], U8, name="tab_planes", tag="planes_then_picks", align_bytes=64)
+        nc.vector.memset(tab_planes[:].bitcast(I32), 0)
+        wh_planes = sb.tile([P, PASSES * H], U8, name="wh_planes", tag="wh_then_z", bufs=2, align_bytes=64)
+        nc.gpsimd.memset(wh_planes[:].bitcast(I32), 0)
+
+        nc.sync.dma_start(offs_sb[:], offs)
+        wh_raw = sb.tile([P, PASSES * 2 * H], U8, name="wh_raw", tag="wh_then_z", bufs=2, align_bytes=64)
+        nc.sync.dma_start(
+            wh_raw[:].bitcast(I32).rearrange("p (a c) -> p a c", a=PASSES),
+            wh_words.bitcast(I32).rearrange("a p c -> p a c"),
+        )
+
+        for quad in range(4):
+            rows = slice(4 * quad, 4 * quad + 4)
+            parts = slice(32 * quad, 32 * quad + 4)
+            nc.sync.dma_start(
+                tab_planes[parts, :].bitcast(I32).rearrange("r (a c) -> r a c", a=PASSES),
+                tab_scales.bitcast(I32)[:, rows, :].rearrange("a r c -> r a c"),
+            )
+        for quad in range(4):
+            rows = slice(4 * quad, 4 * quad + 4)
+            parts = slice(32 * quad, 32 * quad + 4)
+            nc.sync.dma_start(
+                wh_planes[parts, :].bitcast(I32).rearrange("r (a c) -> r a c", a=PASSES),
+                wh_scales.bitcast(I32)[:, rows, :].rearrange("a r c -> r a c"),
+            )
+
+        tab_sb = []
+        for a in range(PASSES):
+            words = sb.tile([P, T], I32, name=f"tab_sb{a}", tag="tab_then_ctx", bufs=2, align_bytes=64)
+            tab_sb.append(words)
+        nc.sync.dma_start(tab_sb[0][:], tab_words[0].rearrange("p c i -> p (c i)").bitcast(I32))
+        nc.sync.dma_start(tab_sb[1][:], tab_words[1].rearrange("p c i -> p (c i)").bitcast(I32))
+        nc.sync.dma_start(pos1_sb[:], pos1)
+        nc.sync.dma_start(pos2_sb[:], pos2)
+        nc.sync.dma_start(pos3_sb[:], pos3)
+        gain_sb = sb.tile([P, PASSES, PACK], F32, name="gain_sb")
+        nc.sync.dma_start(gain_sb[:], gain.rearrange("(b p t) -> p b t", p=P, t=PACK))
+
+        identity = sb.tile([P, P], F32, name="identity")
+        make_identity(nc, identity[:])
+        y_sb = []
+        for slot in range(Y_RING):
+            y_tile = sb.tile([P, M + Y_PAD], F32, name=f"y_sb{slot}")
+            nc.gpsimd.memset(y_tile[:, M:], 0.0)
+            y_sb.append(y_tile)
+
+        def load_weight(w, a):
+            raw = sb.tile([P, PACK, H], F32, name="raw", tag="raw_then_out", bufs=3)
+            nc.sync.dma_start(raw[:], w[HALF * a : HALF * (a + 1), :].rearrange("(p j) c -> p j c", j=PACK))
+            return raw
+
+        def load_ctx(b):
+            rows = sb.tile([P, PACK, S], F32, name=f"ctx_sb{b}", tag="tab_then_ctx", bufs=2, align_bytes=64)
+            nc.sync.dma_start(rows[:], ctx[HALF * b : HALF * (b + 1), :].rearrange("(p t) j -> p t j", t=PACK))
+            return rows
+
+        v_planes = sb.tile([P, PASSES * S], U8, name="v_planes", align_bytes=64)
+        v_codes = sb.tile([P, PASSES * S], U32, name="v_codes", align_bytes=64)
+        for a in range(PASSES):
+            nc.vector.tensor_copy(
+                v_planes[:, S * a : S * (a + 1)], tab_planes[:, T * a : T * (a + 1)].indirect(offs_sb[:])
+            )
+        nc.vector.tensor_copy(v_codes[:, 0:S], tab_sb[0][:].bitcast(U32).indirect(offs_sb[:]))
+
+        wh_codes = sb.tile([P, PASSES * 2 * H], U8, name="wh_codes", align_bytes=64)
+        wh_scale = sb.tile([P, PASSES * H], U8, name="wh_scale", align_bytes=64)
+        nc.vector.tensor_copy(
+            wh_codes[:].bitcast(U16).rearrange("p (g t m) -> p g m t", t=PACK, m=P),
+            wh_raw[:].bitcast(U16).rearrange("p (g m t) -> p g m t", t=PACK, m=P),
+        )
+        nc.vector.tensor_copy(
+            wh_scale[:].rearrange("p (g t m) -> p g m t", t=PACK, m=P),
+            wh_planes[:].rearrange("p (g m t) -> p g m t", t=PACK, m=P),
+        )
+        for half in range(2):
+            nc.vector.tensor_copy(
+                v_codes[:, S + HALF * half : S + HALF * (half + 1)],
+                tab_sb[1][:].bitcast(U32).indirect(offs_sb[:, 32 * half : 32 * (half + 1)]),
+            )
+
+        raw_wc = [load_weight(wc, 0), load_weight(wc, 1)]
+        ctx_sb = [load_ctx(0)]
+        raw_wy0 = load_weight(wy, 0)
+
+        def with_table(acc, codes, planes, fmt, width, u, half):
+            for a in range(PASSES):
+                cols = slice(S * a + HALF * half, S * a + HALF * (half + 1))
+                first = H * a + P * u
+                nc.tensor.matmul_mx(
+                    out=acc[:],
+                    lhsT=codes[:, width * first : width * (first + P)].bitcast(fmt),
+                    lhsT_scale=planes[:, first : first + P],
+                    rhs=v_codes[:, cols].bitcast(FP8X4),
+                    rhs_scale=v_planes[:, cols],
+                    start=(a == 0),
+                    stop=(a == PASSES - 1),
+                )
+
+        h_sb = []
+        picks = []
+        z_codes = sb.tile([P, PASSES * M], U32, name="z_codes", align_bytes=64)
+        z_planes = sb.tile([P, PASSES * M], U8, name="z_planes", align_bytes=64)
+
+        def first_stage(u):
+            t = u % PACK
+            if t == 0:
+                picks1 = sb.tile([P, PACK, M], F32, name="picks1", tag="planes_then_picks", align_bytes=64)
+                picks2 = sb.tile([P, PACK, M], F32, name="picks2")
+                picks.append((picks1, picks2))
+            picks1, picks2 = picks[u // PACK]
+            h_tile = sb.tile([P, S], F32, name=f"h_sb{u}")
+            for half in range(2):
+                acc = psum.tile([P, HALF], F32, name="acc", tag="acc", bufs=3)
+                with_table(acc, wh_codes, wh_scale, FP4X4, 2, u, half)
+                nc.scalar.activation(h_tile[:, HALF * half : HALF * (half + 1)], acc[:], ACT.Copy)
+            nc.vector.tensor_copy(picks1[:, t, :], h_tile[:].indirect(pos1_sb[:]))
+            nc.vector.tensor_copy(picks2[:, t, :], h_tile[:].indirect(pos2_sb[:]))
+            h_sb.append(h_tile)
+
+        def quantise_z(b):
+            picks1, picks2 = picks[b]
+            z_bf = sb.tile([P, M * PACK], BF16, name="z_bf", tag="wh_then_z", bufs=2, align_bytes=64)
+            nc.vector.tensor_tensor(
+                z_bf[:].rearrange("p (c i t) -> p c t i", i=4, t=PACK),
+                picks1[:].rearrange("p t (c i) -> p c t i", i=4),
+                picks2[:].rearrange("p t (c i) -> p c t i", i=4),
+                ALU.max,
+            )
+            nc.vector.quantize_mx(
+                out=z_codes[:, M * b : M * (b + 1)].bitcast(FP8X4),
+                scales=z_planes[:, M * b : M * (b + 1)],
+                in_=z_bf[:],
+            )
+
+        def quantise_weight(raw, a, codes, planes):
+            for b in range(PASSES):
+                rounded = sb.tile([P, HALF * PACK], BF16, name="rounded", tag="rounded", bufs=6, align_bytes=64)
+                nc.scalar.copy(
+                    rounded[:].rearrange("p (t m j) -> p m j t", t=PACK, j=PACK),
+                    raw[:, :, HALF * b : HALF * (b + 1)].rearrange("p j (m t) -> p m j t", t=PACK),
+                )
+                cols = slice(H * a + HALF * b, H * a + HALF * (b + 1))
+                nc.vector.quantize_mx(out=codes[:, cols].bitcast(FP8X4), scales=planes[:, cols], in_=rounded[:])
+
+        wc_codes = sb.tile([P, PASSES * H], U32, name="wc_codes", align_bytes=64)
+        wc_planes = sb.tile([P, PASSES * H], U8, name="wc_planes", align_bytes=64)
+        wy_codes = sb.tile([P, PASSES * H], U32, name="wy_codes", align_bytes=64)
+        wy_planes = sb.tile([P, PASSES * H], U8, name="wy_planes", align_bytes=64)
+
+        def gate(u, half):
+            b, t = divmod(u, PACK)
+            cols = slice(HALF * half, HALF * (half + 1))
+            target = ctx_sb[b][:, t, cols]
+            g = gain_sb[:, b, t : t + 1]
+            acc = psum.tile([P, HALF], F32, name="acc", tag="acc", bufs=3)
+            with_table(acc, wc_codes, wc_planes, FP8X4, 1, u, half)
+            part = sb.tile([P, HALF], F32, name="part", tag="part", bufs=3)
+            terms = [target, part[:]]
+            if ROUTES[u] == "S":
+                nc.scalar.copy(part[:], acc[:])
+                hs = sb.tile([P, HALF], F32, name="hs", tag="hs", bufs=2)
+                nc.scalar.activation(hs[:], h_sb[u][:, cols], ACT.Copy, scale=g)
+                terms.append(hs[:])
+            else:
+                nc.vector.scalar_tensor_tensor(part[:], h_sb[u][:, cols], g, acc[:], ALU.mult, ALU.add)
+            if ROUTES[u] == "V":
+                nc.vector.tensor_tensor(part[:], part[:], target, ALU.add)
+                nc.scalar.activation(target, part[:], ACT.Tanh)
+                return
+            turned = psum.tile([P, HALF], F32, name="turned", tag="turned", bufs=2)
+            for blk in range(HALF // P):
+                bc = slice(P * blk, P * (blk + 1))
+                for n, term in enumerate(terms):
+                    nc.tensor.matmul(
+                        turned[:, bc], term[:, bc], identity[:], start=(n == 0), stop=(n == len(terms) - 1), is_transpose=True
+                    )
+            gate_t = sb.tile([P, HALF], F32, name="gate_t", tag="gate_t", bufs=2)
+            nc.scalar.activation(gate_t[:], turned[:], ACT.Tanh)
+            back = psum.tile([P, HALF], F32, name="back", tag="back", bufs=2)
+            for blk in range(HALF // P):
+                bc = slice(P * blk, P * (blk + 1))
+                nc.tensor.transpose(back[:, bc], gate_t[:, bc], identity[:])
+            nc.scalar.copy(target, back[:])
+
+        def second_stage(u):
+            acc = psum.tile([P, M], F32, name="y_acc", tag="y_acc", bufs=1)
+            for b in range(PASSES):
+                first = H * b + P * u
+                nc.tensor.matmul_mx(
+                    out=acc[:],
+                    lhsT=wy_codes[:, first : first + P].bitcast(FP8X4),
+                    lhsT_scale=wy_planes[:, first : first + P],
+                    rhs=z_codes[:, M * b : M * (b + 1)].bitcast(FP8X4),
+                    rhs_scale=z_planes[:, M * b : M * (b + 1)],
+                    start=(b == 0),
+                    stop=(b == PASSES - 1),
+                )
+            nc.scalar.copy(y_sb[u % Y_RING][:, :M], acc[:])
+
+        out_rows = out.rearrange("(b p t) j -> b t p j", p=P, t=PACK)
+
+        def finish(u):
+            b, t = divmod(u, PACK)
+            result = sb.tile([P, S], F32, name="result", tag="raw_then_out", bufs=3)
+            for half in range(2):
+                cols = slice(HALF * half, HALF * (half + 1))
+                nc.vector.tensor_tensor(
+                    result[:, cols],
+                    y_sb[u % Y_RING][:].indirect(pos3_sb[:, 32 * half : 32 * (half + 1)]),
+                    ctx_sb[b][:, t, cols],
+                    ALU.mult,
+                )
+            for half in range(2):
+                cols = slice(HALF * half, HALF * (half + 1))
+                nc.vector.scalar_tensor_tensor(
+                    result[:, cols], h_sb[u][:, cols], gain_sb[:, b, t : t + 1], result[:, cols], ALU.mult, ALU.add
+                )
+                nc.sync.dma_start(out_rows[b, t][:, cols], result[:, cols])
+
+        for u in range(0, 4):
+            first_stage(u)
+        quantise_z(0)
+        quantise_weight(raw_wc[0], 0, wc_codes, wc_planes)
+        raw_wy1 = load_weight(wy, 1)
+        ctx_sb.append(load_ctx(1))
+        first_stage(4)
+        first_stage(5)
+        quantise_weight(raw_wc[1], 1, wc_codes, wc_planes)
+        first_stage(6)
+        first_stage(7)
+        quantise_z(1)
+        quantise_weight(raw_wy0, 0, wy_codes, wy_planes)
+        gate(0, 0)
+        gate(0, 1)
+        quantise_weight(raw_wy1, 1, wy_codes, wy_planes)
+        second_stage(0)
+        for u in range(1, TILES):
+            gate(u, 0)
+            gate(u, 1)
+            second_stage(u)
+            finish(u - 1)
+        finish(TILES - 1)

@@ -1,7 +1,6 @@
 from contextlib import ExitStack
 
 import concourse.mybir as mybir
-from concourse.masks import make_identity
 
 K, H, T, S, M = 1024, 1024, 4096, 1024, 512
 FLOPS = 2 * K * H * S * 2 + 2 * H * H * M
@@ -24,7 +23,7 @@ TILES = 8
 HALF = 512
 Y_PAD = 16
 Y_RING = 4
-ROUTES = "VVMSSSSS"
+GPSIMD_TILES = 6
 
 
 def tile_list_capsule_bleeding_features_kernel(
@@ -47,41 +46,33 @@ def tile_list_capsule_bleeding_features_kernel(
         nc.gpsimd.memset(wh_planes[:].bitcast(I32), 0)
 
         nc.sync.dma_start(offs_sb[:], offs)
-        wh_raw = sb.tile([P, PASSES * 2 * H], U8, name="wh_raw", tag="wh_then_z", bufs=2, align_bytes=64)
-        nc.sync.dma_start(
-            wh_raw[:].bitcast(I32).rearrange("p (a c) -> p a c", a=PASSES),
-            wh_words.bitcast(I32).rearrange("a p c -> p a c"),
-        )
-
-        for quad in range(4):
-            rows = slice(4 * quad, 4 * quad + 4)
-            parts = slice(32 * quad, 32 * quad + 4)
-            nc.sync.dma_start(
-                tab_planes[parts, :].bitcast(I32).rearrange("r (a c) -> r a c", a=PASSES),
-                tab_scales.bitcast(I32)[:, rows, :].rearrange("a r c -> r a c"),
-            )
-        for quad in range(4):
-            rows = slice(4 * quad, 4 * quad + 4)
-            parts = slice(32 * quad, 32 * quad + 4)
-            nc.sync.dma_start(
-                wh_planes[parts, :].bitcast(I32).rearrange("r (a c) -> r a c", a=PASSES),
-                wh_scales.bitcast(I32)[:, rows, :].rearrange("a r c -> r a c"),
-            )
-
+        nc.sync.dma_start(pos1_sb[:], pos1)
+        nc.sync.dma_start(pos2_sb[:], pos2)
         tab_sb = []
         for a in range(PASSES):
             words = sb.tile([P, T], I32, name=f"tab_sb{a}", tag="tab_then_ctx", bufs=2, align_bytes=64)
             tab_sb.append(words)
-        nc.sync.dma_start(tab_sb[0][:], tab_words[0].rearrange("p c i -> p (c i)").bitcast(I32))
-        nc.sync.dma_start(tab_sb[1][:], tab_words[1].rearrange("p c i -> p (c i)").bitcast(I32))
-        nc.sync.dma_start(pos1_sb[:], pos1)
-        nc.sync.dma_start(pos2_sb[:], pos2)
-        nc.sync.dma_start(pos3_sb[:], pos3)
-        gain_sb = sb.tile([P, PASSES, PACK], F32, name="gain_sb")
-        nc.sync.dma_start(gain_sb[:], gain.rearrange("(b p t) -> p b t", p=P, t=PACK))
+        wh_raw = sb.tile([P, PASSES * 2 * H], U8, name="wh_raw", tag="wh_then_z", bufs=2, align_bytes=64)
 
-        identity = sb.tile([P, P], F32, name="identity")
-        make_identity(nc, identity[:])
+        def load_planes(planes, scales):
+            for quad in range(4):
+                nc.sync.dma_start(
+                    planes[32 * quad : 32 * quad + 4, :].bitcast(I32).rearrange("r (a c) -> r a c", a=PASSES),
+                    scales.bitcast(I32)[:, 4 * quad : 4 * quad + 4, :].rearrange("a r c -> r a c"),
+                )
+
+        nc.sync.dma_start(tab_sb[0][:], tab_words[0].rearrange("p c i -> p (c i)").bitcast(I32))
+        load_planes(tab_planes, tab_scales)
+        nc.sync.dma_start(tab_sb[1][:], tab_words[1].rearrange("p c i -> p (c i)").bitcast(I32))
+        nc.sync.dma_start(
+            wh_raw[:].bitcast(I32).rearrange("p (a c) -> p a c", a=PASSES),
+            wh_words.bitcast(I32).rearrange("a p c -> p a c"),
+        )
+        load_planes(wh_planes, wh_scales)
+
+        def channel_rows(x, b, t):
+            return x.rearrange("(b w t i) n -> b t w (i n)", b=PASSES, t=PACK, i=4)[b, t]
+
         y_sb = []
         for slot in range(Y_RING):
             y_tile = sb.tile([P, M + Y_PAD], F32, name=f"y_sb{slot}")
@@ -89,42 +80,51 @@ def tile_list_capsule_bleeding_features_kernel(
             y_sb.append(y_tile)
 
         def load_weight(w, a):
-            raw = sb.tile([P, PACK, H], F32, name="raw", tag="raw_then_out", bufs=3)
+            raw = sb.tile([P, PACK, H], F32, name="raw", tag="raw_then_out", bufs=3, align_bytes=32)
             nc.sync.dma_start(raw[:], w[HALF * a : HALF * (a + 1), :].rearrange("(p j) c -> p j c", j=PACK))
             return raw
 
-        def load_ctx(b):
-            rows = sb.tile([P, PACK, S], F32, name=f"ctx_sb{b}", tag="tab_then_ctx", bufs=2, align_bytes=64)
-            nc.sync.dma_start(rows[:], ctx[HALF * b : HALF * (b + 1), :].rearrange("(p t) j -> p t j", t=PACK))
+        def load_by_channel(x, b, tag, bufs, align):
+            rows = sb.tile([P, PACK, S], F32, name="rows", tag=tag, bufs=bufs, align_bytes=align)
+            for t in range(PACK):
+                nc.sync.dma_start(rows[:, t, :], channel_rows(x, b, t))
             return rows
 
         v_planes = sb.tile([P, PASSES * S], U8, name="v_planes", align_bytes=64)
         v_codes = sb.tile([P, PASSES * S], U32, name="v_codes", align_bytes=64)
+        nc.vector.tensor_copy(v_codes[:, 0:S], tab_sb[0][:].bitcast(U32).indirect(offs_sb[:]))
         for a in range(PASSES):
             nc.vector.tensor_copy(
                 v_planes[:, S * a : S * (a + 1)], tab_planes[:, T * a : T * (a + 1)].indirect(offs_sb[:])
             )
-        nc.vector.tensor_copy(v_codes[:, 0:S], tab_sb[0][:].bitcast(U32).indirect(offs_sb[:]))
-
-        wh_codes = sb.tile([P, PASSES * 2 * H], U8, name="wh_codes", align_bytes=64)
-        wh_scale = sb.tile([P, PASSES * H], U8, name="wh_scale", align_bytes=64)
-        nc.vector.tensor_copy(
-            wh_codes[:].bitcast(U16).rearrange("p (g t m) -> p g m t", t=PACK, m=P),
-            wh_raw[:].bitcast(U16).rearrange("p (g m t) -> p g m t", t=PACK, m=P),
-        )
-        nc.vector.tensor_copy(
-            wh_scale[:].rearrange("p (g t m) -> p g m t", t=PACK, m=P),
-            wh_planes[:].rearrange("p (g m t) -> p g m t", t=PACK, m=P),
-        )
         for half in range(2):
             nc.vector.tensor_copy(
                 v_codes[:, S + HALF * half : S + HALF * (half + 1)],
                 tab_sb[1][:].bitcast(U32).indirect(offs_sb[:, 32 * half : 32 * (half + 1)]),
             )
+        wh_codes = sb.tile([P, PASSES * 2 * H], U8, name="wh_codes", align_bytes=64)
+        wh_scale = sb.tile([P, PASSES * H], U8, name="wh_scale", align_bytes=64)
+        nc.vector.tensor_copy(
+            wh_codes[:].bitcast(I32).rearrange("p (g t w e) -> p g w t e", t=PACK, w=32, e=2),
+            wh_raw[:].bitcast(I32).rearrange("p (g w t e) -> p g w t e", t=PACK, w=32, e=2),
+        )
+        nc.vector.tensor_copy(
+            wh_scale[:].bitcast(I32).rearrange("p (g t w) -> p g w t", t=PACK, w=32),
+            wh_planes[:].bitcast(I32).rearrange("p (g w t) -> p g w t", t=PACK, w=32),
+        )
 
-        raw_wc = [load_weight(wc, 0), load_weight(wc, 1)]
-        ctx_sb = [load_ctx(0)]
-        raw_wy0 = load_weight(wy, 0)
+        raw_wc = [load_weight(wc, 0)]
+        nc.sync.dma_start(pos3_sb[:], pos3)
+        gain_sb = sb.tile([P, TILES, 8], F32, name="gain_sb")
+        with nc.allow_non_contiguous_dma(reason="one gain value for each partition and tile"):
+            for b in range(PASSES):
+                for t in range(PACK):
+                    nc.gpsimd.dma_start(
+                        gain_sb[:, PACK * b + t, 0:1], gain.rearrange("(b w t i) -> b t w i", b=PASSES, t=PACK, i=4)[b, t]
+                    )
+        raw_wc.append(load_weight(wc, 1))
+        ctx_sb = [load_by_channel(ctx, 0, "tab_then_ctx", 2, 64)]
+        raw_wy0 = load_by_channel(wy, 0, "raw_then_out", 3, 32)
 
         def with_table(acc, codes, planes, fmt, width, u, half):
             for a in range(PASSES):
@@ -154,21 +154,24 @@ def tile_list_capsule_bleeding_features_kernel(
             picks1, picks2 = picks[u // PACK]
             h_tile = sb.tile([P, S], F32, name=f"h_sb{u}")
             for half in range(2):
-                acc = psum.tile([P, HALF], F32, name="acc", tag="acc", bufs=3)
+                acc = psum.tile([P, HALF], F32, name="acc", tag="acc", bufs=6)
                 with_table(acc, wh_codes, wh_scale, FP4X4, 2, u, half)
                 nc.scalar.activation(h_tile[:, HALF * half : HALF * (half + 1)], acc[:], ACT.Copy)
             nc.vector.tensor_copy(picks1[:, t, :], h_tile[:].indirect(pos1_sb[:]))
             nc.vector.tensor_copy(picks2[:, t, :], h_tile[:].indirect(pos2_sb[:]))
             h_sb.append(h_tile)
 
-        def quantise_z(b):
+        def pick_maximum(b):
             picks1, picks2 = picks[b]
-            z_bf = sb.tile([P, M * PACK], BF16, name="z_bf", tag="wh_then_z", bufs=2, align_bytes=64)
-            nc.vector.tensor_tensor(
+            z_rows = sb.tile([P, PACK, M], BF16, name="z_rows", tag="wh_then_z", bufs=2, align_bytes=64)
+            nc.vector.tensor_tensor(z_rows[:], picks1[:], picks2[:], ALU.max)
+            return z_rows
+
+        def quantise_z(b, z_rows):
+            z_bf = sb.tile([P, M * PACK], BF16, name="z_bf", tag="rounded", bufs=6, align_bytes=64)
+            nc.scalar.copy(
                 z_bf[:].rearrange("p (c i t) -> p c t i", i=4, t=PACK),
-                picks1[:].rearrange("p t (c i) -> p c t i", i=4),
-                picks2[:].rearrange("p t (c i) -> p c t i", i=4),
-                ALU.max,
+                z_rows[:].rearrange("p t (c i) -> p c t i", i=4),
             )
             nc.vector.quantize_mx(
                 out=z_codes[:, M * b : M * (b + 1)].bitcast(FP8X4),
@@ -180,8 +183,8 @@ def tile_list_capsule_bleeding_features_kernel(
             for b in range(PASSES):
                 rounded = sb.tile([P, HALF * PACK], BF16, name="rounded", tag="rounded", bufs=6, align_bytes=64)
                 nc.scalar.copy(
-                    rounded[:].rearrange("p (t m j) -> p m j t", t=PACK, j=PACK),
-                    raw[:, :, HALF * b : HALF * (b + 1)].rearrange("p j (m t) -> p m j t", t=PACK),
+                    rounded[:].rearrange("p (t w i j) -> p t w j i", t=PACK, i=4, j=PACK),
+                    raw[:, :, HALF * b : HALF * (b + 1)].rearrange("p j (w t i) -> p t w j i", t=PACK, i=4),
                 )
                 cols = slice(H * a + HALF * b, H * a + HALF * (b + 1))
                 nc.vector.quantize_mx(out=codes[:, cols].bitcast(FP8X4), scales=planes[:, cols], in_=rounded[:])
@@ -195,39 +198,17 @@ def tile_list_capsule_bleeding_features_kernel(
             b, t = divmod(u, PACK)
             cols = slice(HALF * half, HALF * (half + 1))
             target = ctx_sb[b][:, t, cols]
-            g = gain_sb[:, b, t : t + 1]
-            acc = psum.tile([P, HALF], F32, name="acc", tag="acc", bufs=3)
+            g = gain_sb[:, u, 0:1]
+            acc = psum.tile([P, HALF], F32, name="acc", tag="acc", bufs=6)
             with_table(acc, wc_codes, wc_planes, FP8X4, 1, u, half)
-            part = sb.tile([P, HALF], F32, name="part", tag="part", bufs=3)
-            terms = [target, part[:]]
-            if ROUTES[u] == "S":
-                nc.scalar.copy(part[:], acc[:])
-                hs = sb.tile([P, HALF], F32, name="hs", tag="hs", bufs=2)
-                nc.scalar.activation(hs[:], h_sb[u][:, cols], ACT.Copy, scale=g)
-                terms.append(hs[:])
-            else:
-                nc.vector.scalar_tensor_tensor(part[:], h_sb[u][:, cols], g, acc[:], ALU.mult, ALU.add)
-            if ROUTES[u] == "V":
-                nc.vector.tensor_tensor(part[:], part[:], target, ALU.add)
-                nc.scalar.activation(target, part[:], ACT.Tanh)
-                return
-            turned = psum.tile([P, HALF], F32, name="turned", tag="turned", bufs=2)
-            for blk in range(HALF // P):
-                bc = slice(P * blk, P * (blk + 1))
-                for n, term in enumerate(terms):
-                    nc.tensor.matmul(
-                        turned[:, bc], term[:, bc], identity[:], start=(n == 0), stop=(n == len(terms) - 1), is_transpose=True
-                    )
-            gate_t = sb.tile([P, HALF], F32, name="gate_t", tag="gate_t", bufs=2)
-            nc.scalar.activation(gate_t[:], turned[:], ACT.Tanh)
-            back = psum.tile([P, HALF], F32, name="back", tag="back", bufs=2)
-            for blk in range(HALF // P):
-                bc = slice(P * blk, P * (blk + 1))
-                nc.tensor.transpose(back[:, bc], gate_t[:, bc], identity[:])
-            nc.scalar.copy(target, back[:])
+            part = sb.tile([P, HALF], F32, name="part", tag="part", bufs=8)
+            nc.vector.scalar_tensor_tensor(part[:], h_sb[u][:, cols], g, acc[:], ALU.mult, ALU.add)
+            adder = nc.gpsimd if u < GPSIMD_TILES else nc.vector
+            adder.tensor_tensor(target, part[:], target, ALU.add)
+            nc.scalar.activation(target, target, ACT.Tanh)
 
         def second_stage(u):
-            acc = psum.tile([P, M], F32, name="y_acc", tag="y_acc", bufs=1)
+            acc = psum.tile([P, M], F32, name="y_acc", tag="y_acc", bufs=2)
             for b in range(PASSES):
                 first = H * b + P * u
                 nc.tensor.matmul_mx(
@@ -241,11 +222,11 @@ def tile_list_capsule_bleeding_features_kernel(
                 )
             nc.scalar.copy(y_sb[u % Y_RING][:, :M], acc[:])
 
-        out_rows = out.rearrange("(b p t) j -> b t p j", p=P, t=PACK)
+        out_rows = out.rearrange("(b w t i) j -> b t w i j", b=PASSES, t=PACK, i=4)
 
         def finish(u):
             b, t = divmod(u, PACK)
-            result = sb.tile([P, S], F32, name="result", tag="raw_then_out", bufs=3)
+            result = sb.tile([P, S], F32, name="result", tag="raw_then_out", bufs=3, align_bytes=32)
             for half in range(2):
                 cols = slice(HALF * half, HALF * (half + 1))
                 nc.vector.tensor_tensor(
@@ -257,30 +238,36 @@ def tile_list_capsule_bleeding_features_kernel(
             for half in range(2):
                 cols = slice(HALF * half, HALF * (half + 1))
                 nc.vector.scalar_tensor_tensor(
-                    result[:, cols], h_sb[u][:, cols], gain_sb[:, b, t : t + 1], result[:, cols], ALU.mult, ALU.add
+                    result[:, cols], h_sb[u][:, cols], gain_sb[:, u, 0:1], result[:, cols], ALU.mult, ALU.add
                 )
-                nc.sync.dma_start(out_rows[b, t][:, cols], result[:, cols])
+                nc.sync.dma_start(out_rows[b, t][:, :, cols], result[:, cols])
+
+        def gates(u):
+            gate(u, 0)
+            gate(u, 1)
 
         for u in range(0, 4):
             first_stage(u)
-        quantise_z(0)
+        z_rows0 = pick_maximum(0)
         quantise_weight(raw_wc[0], 0, wc_codes, wc_planes)
-        raw_wy1 = load_weight(wy, 1)
-        ctx_sb.append(load_ctx(1))
+        raw_wy1 = load_by_channel(wy, 1, "raw_then_out", 3, 32)
+        ctx_sb.append(load_by_channel(ctx, 1, "tab_then_ctx", 2, 64))
         first_stage(4)
-        first_stage(5)
         quantise_weight(raw_wc[1], 1, wc_codes, wc_planes)
-        first_stage(6)
-        first_stage(7)
-        quantise_z(1)
+        for u in range(5, TILES):
+            first_stage(u)
+        z_rows1 = pick_maximum(1)
+        gates(0)
         quantise_weight(raw_wy0, 0, wy_codes, wy_planes)
-        gate(0, 0)
-        gate(0, 1)
+        quantise_z(0, z_rows0)
+        gates(1)
         quantise_weight(raw_wy1, 1, wy_codes, wy_planes)
-        second_stage(0)
-        for u in range(1, TILES):
-            gate(u, 0)
-            gate(u, 1)
+        quantise_z(1, z_rows1)
+        for u in range(Y_RING):
             second_stage(u)
-            finish(u - 1)
-        finish(TILES - 1)
+        for u in range(2, TILES):
+            gates(u)
+        for u in range(TILES):
+            finish(u)
+            if u + Y_RING < TILES:
+                second_stage(u + Y_RING)

@@ -1,6 +1,7 @@
 from contextlib import ExitStack
 
 import concourse.mybir as mybir
+from concourse.masks import make_identity
 
 K, H, T, S, M = 1024, 1024, 4096, 1024, 512
 FLOPS = 2 * K * H * S * 2 + 2 * H * H * M
@@ -21,9 +22,9 @@ PACK = 4
 PASSES = 2
 TILES = 8
 HALF = 512
-Y_PAD = 16
+Y_PAD = 528
 Y_RING = 4
-GPSIMD_TILES = 6
+VECTOR_TILES = 5
 
 
 def tile_list_capsule_bleeding_features_kernel(
@@ -63,16 +64,18 @@ def tile_list_capsule_bleeding_features_kernel(
 
         nc.sync.dma_start(tab_sb[0][:], tab_words[0].rearrange("p c i -> p (c i)").bitcast(I32))
         load_planes(tab_planes, tab_scales)
-        nc.sync.dma_start(tab_sb[1][:], tab_words[1].rearrange("p c i -> p (c i)").bitcast(I32))
         nc.sync.dma_start(
             wh_raw[:].bitcast(I32).rearrange("p (a c) -> p a c", a=PASSES),
             wh_words.bitcast(I32).rearrange("a p c -> p a c"),
         )
         load_planes(wh_planes, wh_scales)
+        nc.sync.dma_start(tab_sb[1][:], tab_words[1].rearrange("p c i -> p (c i)").bitcast(I32))
 
         def channel_rows(x, b, t):
             return x.rearrange("(b w t i) n -> b t w (i n)", b=PASSES, t=PACK, i=4)[b, t]
 
+        identity = sb.tile([P, P], F32, name="identity")
+        make_identity(nc, identity[:])
         y_sb = []
         for slot in range(Y_RING):
             y_tile = sb.tile([P, M + Y_PAD], F32, name=f"y_sb{slot}")
@@ -97,11 +100,6 @@ def tile_list_capsule_bleeding_features_kernel(
             nc.vector.tensor_copy(
                 v_planes[:, S * a : S * (a + 1)], tab_planes[:, T * a : T * (a + 1)].indirect(offs_sb[:])
             )
-        for half in range(2):
-            nc.vector.tensor_copy(
-                v_codes[:, S + HALF * half : S + HALF * (half + 1)],
-                tab_sb[1][:].bitcast(U32).indirect(offs_sb[:, 32 * half : 32 * (half + 1)]),
-            )
         wh_codes = sb.tile([P, PASSES * 2 * H], U8, name="wh_codes", align_bytes=64)
         wh_scale = sb.tile([P, PASSES * H], U8, name="wh_scale", align_bytes=64)
         nc.vector.tensor_copy(
@@ -112,16 +110,25 @@ def tile_list_capsule_bleeding_features_kernel(
             wh_scale[:].bitcast(I32).rearrange("p (g t w) -> p g w t", t=PACK, w=32),
             wh_planes[:].bitcast(I32).rearrange("p (g w t) -> p g w t", t=PACK, w=32),
         )
+        for half in range(2):
+            nc.vector.tensor_copy(
+                v_codes[:, S + HALF * half : S + HALF * (half + 1)],
+                tab_sb[1][:].bitcast(U32).indirect(offs_sb[:, 32 * half : 32 * (half + 1)]),
+            )
 
         raw_wc = [load_weight(wc, 0)]
         nc.sync.dma_start(pos3_sb[:], pos3)
-        gain_sb = sb.tile([P, TILES, 8], F32, name="gain_sb")
-        with nc.allow_non_contiguous_dma(reason="one gain value for each partition and tile"):
-            for b in range(PASSES):
-                for t in range(PACK):
-                    nc.gpsimd.dma_start(
-                        gain_sb[:, PACK * b + t, 0:1], gain.rearrange("(b w t i) -> b t w i", b=PASSES, t=PACK, i=4)[b, t]
-                    )
+        gain_rows = sb.tile([P, P], F32, name="gain_rows")
+        nc.gpsimd.memset(gain_rows[:], 0.0)
+        for b in range(PASSES):
+            nc.sync.dma_start(
+                gain_rows[PACK * b : PACK * (b + 1), :].rearrange("t (w i) -> t w i", i=4),
+                gain.rearrange("(b w t i) -> b t w i", b=PASSES, t=PACK, i=4)[b],
+            )
+        gain_turned = psum.tile([P, HALF], F32, name="gain_turned", tag="back", bufs=1)
+        nc.tensor.transpose(gain_turned[:, :P], gain_rows[:], identity[:])
+        gain_sb = sb.tile([P, TILES], F32, name="gain_sb")
+        nc.scalar.copy(gain_sb[:], gain_turned[:, :TILES])
         raw_wc.append(load_weight(wc, 1))
         ctx_sb = [load_by_channel(ctx, 0, "tab_then_ctx", 2, 64)]
         raw_wy0 = load_by_channel(wy, 0, "raw_then_out", 3, 32)
@@ -154,7 +161,7 @@ def tile_list_capsule_bleeding_features_kernel(
             picks1, picks2 = picks[u // PACK]
             h_tile = sb.tile([P, S], F32, name=f"h_sb{u}")
             for half in range(2):
-                acc = psum.tile([P, HALF], F32, name="acc", tag="acc", bufs=6)
+                acc = psum.tile([P, HALF], F32, name="acc", tag="acc", bufs=3)
                 with_table(acc, wh_codes, wh_scale, FP4X4, 2, u, half)
                 nc.scalar.activation(h_tile[:, HALF * half : HALF * (half + 1)], acc[:], ACT.Copy)
             nc.vector.tensor_copy(picks1[:, t, :], h_tile[:].indirect(pos1_sb[:]))
@@ -168,7 +175,7 @@ def tile_list_capsule_bleeding_features_kernel(
             return z_rows
 
         def quantise_z(b, z_rows):
-            z_bf = sb.tile([P, M * PACK], BF16, name="z_bf", tag="rounded", bufs=6, align_bytes=64)
+            z_bf = sb.tile([P, M * PACK], BF16, name="z_bf", tag="rounded", bufs=5, align_bytes=64)
             nc.scalar.copy(
                 z_bf[:].rearrange("p (c i t) -> p c t i", i=4, t=PACK),
                 z_rows[:].rearrange("p t (c i) -> p c t i", i=4),
@@ -181,7 +188,7 @@ def tile_list_capsule_bleeding_features_kernel(
 
         def quantise_weight(raw, a, codes, planes):
             for b in range(PASSES):
-                rounded = sb.tile([P, HALF * PACK], BF16, name="rounded", tag="rounded", bufs=6, align_bytes=64)
+                rounded = sb.tile([P, HALF * PACK], BF16, name="rounded", tag="rounded", bufs=5, align_bytes=64)
                 nc.scalar.copy(
                     rounded[:].rearrange("p (t w i j) -> p t w j i", t=PACK, i=4, j=PACK),
                     raw[:, :, HALF * b : HALF * (b + 1)].rearrange("p j (w t i) -> p t w j i", t=PACK, i=4),
@@ -194,21 +201,49 @@ def tile_list_capsule_bleeding_features_kernel(
         wy_codes = sb.tile([P, PASSES * H], U32, name="wy_codes", align_bytes=64)
         wy_planes = sb.tile([P, PASSES * H], U8, name="wy_planes", align_bytes=64)
 
-        def gate(u, half):
+        def gate_on_vector(u):
             b, t = divmod(u, PACK)
-            cols = slice(HALF * half, HALF * (half + 1))
-            target = ctx_sb[b][:, t, cols]
-            g = gain_sb[:, u, 0:1]
-            acc = psum.tile([P, HALF], F32, name="acc", tag="acc", bufs=6)
-            with_table(acc, wc_codes, wc_planes, FP8X4, 1, u, half)
-            part = sb.tile([P, HALF], F32, name="part", tag="part", bufs=8)
-            nc.vector.scalar_tensor_tensor(part[:], h_sb[u][:, cols], g, acc[:], ALU.mult, ALU.add)
-            adder = nc.gpsimd if u < GPSIMD_TILES else nc.vector
-            adder.tensor_tensor(target, part[:], target, ALU.add)
+            target = ctx_sb[b][:, t, :]
+            part = sb.tile([P, S], F32, name="part", tag="part", bufs=2)
+            for half in range(2):
+                cols = slice(HALF * half, HALF * (half + 1))
+                acc = psum.tile([P, HALF], F32, name="acc", tag="acc", bufs=3)
+                with_table(acc, wc_codes, wc_planes, FP8X4, 1, u, half)
+                nc.vector.scalar_tensor_tensor(
+                    part[:, cols], h_sb[u][:, cols], gain_sb[:, u : u + 1], acc[:], ALU.mult, ALU.add
+                )
+            nc.vector.tensor_tensor(target, part[:], target, ALU.add)
             nc.scalar.activation(target, target, ACT.Tanh)
 
+        def gate_by_transposes(u):
+            b, t = divmod(u, PACK)
+            for half in range(2):
+                cols = slice(HALF * half, HALF * (half + 1))
+                target = ctx_sb[b][:, t, cols]
+                acc = psum.tile([P, HALF], F32, name="look_acc", tag="look_acc", bufs=1)
+                with_table(acc, wc_codes, wc_planes, FP8X4, 1, u, half)
+                look = sb.tile([P, HALF], F32, name="look", tag="look", bufs=2)
+                nc.scalar.copy(look[:], acc[:])
+                hs = sb.tile([P, HALF], F32, name="hs", tag="hs", bufs=2)
+                nc.scalar.activation(hs[:], h_sb[u][:, cols], ACT.Copy, scale=gain_sb[:, u : u + 1])
+                terms = [target, look[:], hs[:]]
+                turned = psum.tile([P, HALF], F32, name="turned", tag="turned", bufs=2)
+                for blk in range(HALF // P):
+                    bc = slice(P * blk, P * (blk + 1))
+                    for n, term in enumerate(terms):
+                        nc.tensor.matmul(
+                            turned[:, bc], term[:, bc], identity[:], start=(n == 0), stop=(n == 2), is_transpose=True
+                        )
+                gate_t = sb.tile([P, HALF], F32, name="gate_t", tag="gate_t", bufs=2)
+                nc.scalar.activation(gate_t[:], turned[:], ACT.Tanh)
+                back = psum.tile([P, HALF], F32, name="back", tag="back", bufs=1)
+                for blk in range(HALF // P):
+                    bc = slice(P * blk, P * (blk + 1))
+                    nc.tensor.transpose(back[:, bc], gate_t[:, bc], identity[:])
+                nc.scalar.copy(target, back[:])
+
         def second_stage(u):
-            acc = psum.tile([P, M], F32, name="y_acc", tag="y_acc", bufs=2)
+            acc = psum.tile([P, M], F32, name="y_acc", tag="y_acc", bufs=1)
             for b in range(PASSES):
                 first = H * b + P * u
                 nc.tensor.matmul_mx(
@@ -227,24 +262,28 @@ def tile_list_capsule_bleeding_features_kernel(
         def finish(u):
             b, t = divmod(u, PACK)
             result = sb.tile([P, S], F32, name="result", tag="raw_then_out", bufs=3, align_bytes=32)
-            for half in range(2):
-                cols = slice(HALF * half, HALF * (half + 1))
+            pieces = 2 if u == TILES - 1 else 1
+            width = S // pieces
+            for piece in range(pieces):
+                cols = slice(width * piece, width * (piece + 1))
                 nc.vector.tensor_tensor(
                     result[:, cols],
-                    y_sb[u % Y_RING][:].indirect(pos3_sb[:, 32 * half : 32 * (half + 1)]),
+                    y_sb[u % Y_RING][:].indirect(pos3_sb[:, width // 16 * piece : width // 16 * (piece + 1)]),
                     ctx_sb[b][:, t, cols],
                     ALU.mult,
                 )
-            for half in range(2):
-                cols = slice(HALF * half, HALF * (half + 1))
+            return result
+
+        def add_and_store(u, result):
+            b, t = divmod(u, PACK)
+            pieces = 2 if u == TILES - 1 else 1
+            width = S // pieces
+            for piece in range(pieces):
+                cols = slice(width * piece, width * (piece + 1))
                 nc.vector.scalar_tensor_tensor(
-                    result[:, cols], h_sb[u][:, cols], gain_sb[:, u, 0:1], result[:, cols], ALU.mult, ALU.add
+                    result[:, cols], h_sb[u][:, cols], gain_sb[:, u : u + 1], result[:, cols], ALU.mult, ALU.add
                 )
                 nc.sync.dma_start(out_rows[b, t][:, :, cols], result[:, cols])
-
-        def gates(u):
-            gate(u, 0)
-            gate(u, 1)
 
         for u in range(0, 4):
             first_stage(u)
@@ -257,17 +296,25 @@ def tile_list_capsule_bleeding_features_kernel(
         for u in range(5, TILES):
             first_stage(u)
         z_rows1 = pick_maximum(1)
-        gates(0)
         quantise_weight(raw_wy0, 0, wy_codes, wy_planes)
         quantise_z(0, z_rows0)
-        gates(1)
         quantise_weight(raw_wy1, 1, wy_codes, wy_planes)
         quantise_z(1, z_rows1)
         for u in range(Y_RING):
             second_stage(u)
-        for u in range(2, TILES):
-            gates(u)
-        for u in range(TILES):
-            finish(u)
-            if u + Y_RING < TILES:
-                second_stage(u + Y_RING)
+        gate_on_vector(0)
+        gate_by_transposes(5)
+        gate_on_vector(1)
+        gate_on_vector(2)
+        gate_by_transposes(6)
+        gate_on_vector(3)
+        gate_on_vector(4)
+        gate_by_transposes(7)
+        pending = finish(0)
+        for u in range(1, TILES):
+            if u - 1 + Y_RING < TILES:
+                second_stage(u - 1 + Y_RING)
+            result = finish(u)
+            add_and_store(u - 1, pending)
+            pending = result
+        add_and_store(TILES - 1, pending)

from contextlib import ExitStack

import concourse.mybir as mybir
from concourse.masks import make_identity

K, H, T, S, M = 1024, 1024, 4096, 1024, 512
FLOPS = 2 * K * H * S * 2 + 2 * H * H * M

F32 = mybir.dt.float32
BF16 = mybir.dt.bfloat16
I32 = mybir.dt.int32
U32 = mybir.dt.uint32
U16 = mybir.dt.uint16
U8 = mybir.dt.uint8
FP8X4 = mybir.dt.float8_e4m3fn_x4
FP4X4 = mybir.dt.float4_e2m1fn_x4
ALU = mybir.AluOpType
ACT = mybir.ActivationFunctionType

P = 128
PACK = 4
PASSES = 2
TILES = 8
HALF = 512
Y_PAD = 528
Y_RING = 4
VECTOR_TILES = 5


def tile_list_capsule_bleeding_features_kernel(
    tc, tab_words, tab_scales, offs, pos1, pos2, pos3, wc, ctx, wh_words, wh_scales, wy, gain, out
):
    nc = tc.nc
    with ExitStack() as stack:
        lists = stack.enter_context(tc.tile_pool(name="lists", bufs=1))
        sb = stack.enter_context(tc.tile_pool(name="sb", bufs=1))
        psum = stack.enter_context(tc.psum_pool(name="psum", bufs=1))

        offs_sb = lists.tile([P, S // 16], U16, name="offs_sb")
        pos1_sb = lists.tile([P, M // 16], U16, name="pos1_sb")
        pos2_sb = lists.tile([P, M // 16], U16, name="pos2_sb")
        pos3_sb = lists.tile([P, S // 16], U16, name="pos3_sb")

        tab_planes = sb.tile([P, PASSES * T], U8, name="tab_planes", tag="planes_then_picks", align_bytes=64)
        nc.vector.memset(tab_planes[:].bitcast(I32), 0)
        wh_planes = sb.tile([P, PASSES * H], U8, name="wh_planes", tag="wh_then_z", bufs=2, align_bytes=64)
        nc.gpsimd.memset(wh_planes[:].bitcast(I32), 0)

        nc.sync.dma_start(offs_sb[:], offs)
        nc.sync.dma_start(pos1_sb[:], pos1)
        nc.sync.dma_start(pos2_sb[:], pos2)
        tab_sb = []
        for a in range(PASSES):
            words = sb.tile([P, T], I32, name=f"tab_sb{a}", tag="tab_then_ctx", bufs=2, align_bytes=64)
            tab_sb.append(words)
        wh_raw = sb.tile([P, PASSES * 2 * H], U8, name="wh_raw", tag="wh_then_z", bufs=2, align_bytes=64)

        def load_planes(planes, scales):
            for quad in range(4):
                nc.sync.dma_start(
                    planes[32 * quad : 32 * quad + 4, :].bitcast(I32).rearrange("r (a c) -> r a c", a=PASSES),
                    scales.bitcast(I32)[:, 4 * quad : 4 * quad + 4, :].rearrange("a r c -> r a c"),
                )

        nc.sync.dma_start(tab_sb[0][:], tab_words[0].rearrange("p c i -> p (c i)").bitcast(I32))
        load_planes(tab_planes, tab_scales)
        nc.sync.dma_start(
            wh_raw[:].bitcast(I32).rearrange("p (a c) -> p a c", a=PASSES),
            wh_words.bitcast(I32).rearrange("a p c -> p a c"),
        )
        load_planes(wh_planes, wh_scales)
        nc.sync.dma_start(tab_sb[1][:], tab_words[1].rearrange("p c i -> p (c i)").bitcast(I32))

        def channel_rows(x, b, t):
            return x.rearrange("(b w t i) n -> b t w (i n)", b=PASSES, t=PACK, i=4)[b, t]

        identity = sb.tile([P, P], F32, name="identity")
        make_identity(nc, identity[:])
        y_sb = []
        for slot in range(Y_RING):
            y_tile = sb.tile([P, M + Y_PAD], F32, name=f"y_sb{slot}")
            nc.gpsimd.memset(y_tile[:, M:], 0.0)
            y_sb.append(y_tile)

        def load_weight(w, a):
            raw = sb.tile([P, PACK, H], F32, name="raw", tag="raw_then_out", bufs=3, align_bytes=32)
            nc.sync.dma_start(raw[:], w[HALF * a : HALF * (a + 1), :].rearrange("(p j) c -> p j c", j=PACK))
            return raw

        def load_by_channel(x, b, tag, bufs, align):
            rows = sb.tile([P, PACK, S], F32, name="rows", tag=tag, bufs=bufs, align_bytes=align)
            for t in range(PACK):
                nc.sync.dma_start(rows[:, t, :], channel_rows(x, b, t))
            return rows

        v_planes = sb.tile([P, PASSES * S], U8, name="v_planes", align_bytes=64)
        v_codes = sb.tile([P, PASSES * S], U32, name="v_codes", align_bytes=64)
        nc.vector.tensor_copy(v_codes[:, 0:S], tab_sb[0][:].bitcast(U32).indirect(offs_sb[:]))
        for a in range(PASSES):
            nc.vector.tensor_copy(
                v_planes[:, S * a : S * (a + 1)], tab_planes[:, T * a : T * (a + 1)].indirect(offs_sb[:])
            )
        wh_codes = sb.tile([P, PASSES * 2 * H], U8, name="wh_codes", align_bytes=64)
        wh_scale = sb.tile([P, PASSES * H], U8, name="wh_scale", align_bytes=64)
        nc.vector.tensor_copy(
            wh_codes[:].bitcast(I32).rearrange("p (g t w e) -> p g w t e", t=PACK, w=32, e=2),
            wh_raw[:].bitcast(I32).rearrange("p (g w t e) -> p g w t e", t=PACK, w=32, e=2),
        )
        nc.vector.tensor_copy(
            wh_scale[:].bitcast(I32).rearrange("p (g t w) -> p g w t", t=PACK, w=32),
            wh_planes[:].bitcast(I32).rearrange("p (g w t) -> p g w t", t=PACK, w=32),
        )
        for half in range(2):
            nc.vector.tensor_copy(
                v_codes[:, S + HALF * half : S + HALF * (half + 1)],
                tab_sb[1][:].bitcast(U32).indirect(offs_sb[:, 32 * half : 32 * (half + 1)]),
            )

        raw_wc = [load_weight(wc, 0)]
        nc.sync.dma_start(pos3_sb[:], pos3)
        gain_rows = sb.tile([P, P], F32, name="gain_rows")
        nc.gpsimd.memset(gain_rows[:], 0.0)
        for b in range(PASSES):
            nc.sync.dma_start(
                gain_rows[PACK * b : PACK * (b + 1), :].rearrange("t (w i) -> t w i", i=4),
                gain.rearrange("(b w t i) -> b t w i", b=PASSES, t=PACK, i=4)[b],
            )
        gain_turned = psum.tile([P, HALF], F32, name="gain_turned", tag="back", bufs=1)
        nc.tensor.transpose(gain_turned[:, :P], gain_rows[:], identity[:])
        gain_sb = sb.tile([P, TILES], F32, name="gain_sb")
        nc.scalar.copy(gain_sb[:], gain_turned[:, :TILES])
        raw_wc.append(load_weight(wc, 1))
        ctx_sb = [load_by_channel(ctx, 0, "tab_then_ctx", 2, 64)]
        raw_wy0 = load_by_channel(wy, 0, "raw_then_out", 3, 32)

        def with_table(acc, codes, planes, fmt, width, u, half):
            for a in range(PASSES):
                cols = slice(S * a + HALF * half, S * a + HALF * (half + 1))
                first = H * a + P * u
                nc.tensor.matmul_mx(
                    out=acc[:],
                    lhsT=codes[:, width * first : width * (first + P)].bitcast(fmt),
                    lhsT_scale=planes[:, first : first + P],
                    rhs=v_codes[:, cols].bitcast(FP8X4),
                    rhs_scale=v_planes[:, cols],
                    start=(a == 0),
                    stop=(a == PASSES - 1),
                )

        h_sb = []
        picks = []
        z_codes = sb.tile([P, PASSES * M], U32, name="z_codes", align_bytes=64)
        z_planes = sb.tile([P, PASSES * M], U8, name="z_planes", align_bytes=64)

        def first_stage(u):
            t = u % PACK
            if t == 0:
                picks1 = sb.tile([P, PACK, M], F32, name="picks1", tag="planes_then_picks", align_bytes=64)
                picks2 = sb.tile([P, PACK, M], F32, name="picks2")
                picks.append((picks1, picks2))
            picks1, picks2 = picks[u // PACK]
            h_tile = sb.tile([P, S], F32, name=f"h_sb{u}")
            for half in range(2):
                acc = psum.tile([P, HALF], F32, name="acc", tag="acc", bufs=3)
                with_table(acc, wh_codes, wh_scale, FP4X4, 2, u, half)
                nc.scalar.activation(h_tile[:, HALF * half : HALF * (half + 1)], acc[:], ACT.Copy)
            nc.vector.tensor_copy(picks1[:, t, :], h_tile[:].indirect(pos1_sb[:]))
            nc.vector.tensor_copy(picks2[:, t, :], h_tile[:].indirect(pos2_sb[:]))
            h_sb.append(h_tile)

        def pick_maximum(b):
            picks1, picks2 = picks[b]
            z_rows = sb.tile([P, PACK, M], BF16, name="z_rows", tag="wh_then_z", bufs=2, align_bytes=64)
            nc.vector.tensor_tensor(z_rows[:], picks1[:], picks2[:], ALU.max)
            return z_rows

        def quantise_z(b, z_rows):
            z_bf = sb.tile([P, M * PACK], BF16, name="z_bf", tag="rounded", bufs=5, align_bytes=64)
            nc.scalar.copy(
                z_bf[:].rearrange("p (c i t) -> p c t i", i=4, t=PACK),
                z_rows[:].rearrange("p t (c i) -> p c t i", i=4),
            )
            nc.vector.quantize_mx(
                out=z_codes[:, M * b : M * (b + 1)].bitcast(FP8X4),
                scales=z_planes[:, M * b : M * (b + 1)],
                in_=z_bf[:],
            )

        def quantise_weight(raw, a, codes, planes):
            for b in range(PASSES):
                rounded = sb.tile([P, HALF * PACK], BF16, name="rounded", tag="rounded", bufs=5, align_bytes=64)
                nc.scalar.copy(
                    rounded[:].rearrange("p (t w i j) -> p t w j i", t=PACK, i=4, j=PACK),
                    raw[:, :, HALF * b : HALF * (b + 1)].rearrange("p j (w t i) -> p t w j i", t=PACK, i=4),
                )
                cols = slice(H * a + HALF * b, H * a + HALF * (b + 1))
                nc.vector.quantize_mx(out=codes[:, cols].bitcast(FP8X4), scales=planes[:, cols], in_=rounded[:])

        wc_codes = sb.tile([P, PASSES * H], U32, name="wc_codes", align_bytes=64)
        wc_planes = sb.tile([P, PASSES * H], U8, name="wc_planes", align_bytes=64)
        wy_codes = sb.tile([P, PASSES * H], U32, name="wy_codes", align_bytes=64)
        wy_planes = sb.tile([P, PASSES * H], U8, name="wy_planes", align_bytes=64)

        def gate_on_vector(u):
            b, t = divmod(u, PACK)
            target = ctx_sb[b][:, t, :]
            part = sb.tile([P, S], F32, name="part", tag="part", bufs=2)
            for half in range(2):
                cols = slice(HALF * half, HALF * (half + 1))
                acc = psum.tile([P, HALF], F32, name="acc", tag="acc", bufs=3)
                with_table(acc, wc_codes, wc_planes, FP8X4, 1, u, half)
                nc.vector.scalar_tensor_tensor(
                    part[:, cols], h_sb[u][:, cols], gain_sb[:, u : u + 1], acc[:], ALU.mult, ALU.add
                )
            nc.vector.tensor_tensor(target, part[:], target, ALU.add)
            nc.scalar.activation(target, target, ACT.Tanh)

        def gate_by_transposes(u):
            b, t = divmod(u, PACK)
            for half in range(2):
                cols = slice(HALF * half, HALF * (half + 1))
                target = ctx_sb[b][:, t, cols]
                acc = psum.tile([P, HALF], F32, name="look_acc", tag="look_acc", bufs=1)
                with_table(acc, wc_codes, wc_planes, FP8X4, 1, u, half)
                look = sb.tile([P, HALF], F32, name="look", tag="look", bufs=2)
                nc.scalar.copy(look[:], acc[:])
                hs = sb.tile([P, HALF], F32, name="hs", tag="hs", bufs=2)
                nc.scalar.activation(hs[:], h_sb[u][:, cols], ACT.Copy, scale=gain_sb[:, u : u + 1])
                terms = [target, look[:], hs[:]]
                turned = psum.tile([P, HALF], F32, name="turned", tag="turned", bufs=2)
                for blk in range(HALF // P):
                    bc = slice(P * blk, P * (blk + 1))
                    for n, term in enumerate(terms):
                        nc.tensor.matmul(
                            turned[:, bc], term[:, bc], identity[:], start=(n == 0), stop=(n == 2), is_transpose=True
                        )
                gate_t = sb.tile([P, HALF], F32, name="gate_t", tag="gate_t", bufs=2)
                nc.scalar.activation(gate_t[:], turned[:], ACT.Tanh)
                back = psum.tile([P, HALF], F32, name="back", tag="back", bufs=1)
                for blk in range(HALF // P):
                    bc = slice(P * blk, P * (blk + 1))
                    nc.tensor.transpose(back[:, bc], gate_t[:, bc], identity[:])
                nc.scalar.copy(target, back[:])

        def second_stage(u):
            acc = psum.tile([P, M], F32, name="y_acc", tag="y_acc", bufs=1)
            for b in range(PASSES):
                first = H * b + P * u
                nc.tensor.matmul_mx(
                    out=acc[:],
                    lhsT=wy_codes[:, first : first + P].bitcast(FP8X4),
                    lhsT_scale=wy_planes[:, first : first + P],
                    rhs=z_codes[:, M * b : M * (b + 1)].bitcast(FP8X4),
                    rhs_scale=z_planes[:, M * b : M * (b + 1)],
                    start=(b == 0),
                    stop=(b == PASSES - 1),
                )
            nc.scalar.copy(y_sb[u % Y_RING][:, :M], acc[:])

        out_rows = out.rearrange("(b w t i) j -> b t w i j", b=PASSES, t=PACK, i=4)

        def finish(u):
            b, t = divmod(u, PACK)
            result = sb.tile([P, S], F32, name="result", tag="raw_then_out", bufs=3, align_bytes=32)
            pieces = 2 if u == TILES - 1 else 1
            width = S // pieces
            for piece in range(pieces):
                cols = slice(width * piece, width * (piece + 1))
                nc.vector.tensor_tensor(
                    result[:, cols],
                    y_sb[u % Y_RING][:].indirect(pos3_sb[:, width // 16 * piece : width // 16 * (piece + 1)]),
                    ctx_sb[b][:, t, cols],
                    ALU.mult,
                )
            return result

        def add_and_store(u, result):
            b, t = divmod(u, PACK)
            pieces = 2 if u == TILES - 1 else 1
            width = S // pieces
            for piece in range(pieces):
                cols = slice(width * piece, width * (piece + 1))
                nc.vector.scalar_tensor_tensor(
                    result[:, cols], h_sb[u][:, cols], gain_sb[:, u : u + 1], result[:, cols], ALU.mult, ALU.add
                )
                nc.sync.dma_start(out_rows[b, t][:, :, cols], result[:, cols])

        for u in range(0, 4):
            first_stage(u)
        z_rows0 = pick_maximum(0)
        quantise_weight(raw_wc[0], 0, wc_codes, wc_planes)
        raw_wy1 = load_by_channel(wy, 1, "raw_then_out", 3, 32)
        ctx_sb.append(load_by_channel(ctx, 1, "tab_then_ctx", 2, 64))
        first_stage(4)
        quantise_weight(raw_wc[1], 1, wc_codes, wc_planes)
        for u in range(5, TILES):
            first_stage(u)
        z_rows1 = pick_maximum(1)
        quantise_weight(raw_wy0, 0, wy_codes, wy_planes)
        quantise_z(0, z_rows0)
        quantise_weight(raw_wy1, 1, wy_codes, wy_planes)
        quantise_z(1, z_rows1)
        for u in range(Y_RING):
            second_stage(u)
        gate_on_vector(0)
        gate_by_transposes(5)
        gate_on_vector(1)
        gate_on_vector(2)
        gate_by_transposes(6)
        gate_on_vector(3)
        gate_on_vector(4)
        gate_by_transposes(7)
        pending = finish(0)
        for u in range(1, TILES):
            if u - 1 + Y_RING < TILES:
                second_stage(u - 1 + Y_RING)
            result = finish(u)
            add_and_store(u - 1, pending)
            pending = result
        add_and_store(TILES - 1, pending)
